import numpy as np
import ml_dtypes


def mxq(x, axis, fmt="e4m3"):
    dtype, down = {"e4m3": (ml_dtypes.float8_e4m3fn, 7), "e5m2": (ml_dtypes.float8_e5m2, 14)}[fmt]
    v = np.moveaxis(np.asarray(x, np.float32).astype(ml_dtypes.bfloat16).astype(np.float64), axis, -1)
    blocks = v.reshape(v.shape[:-1] + (-1, 32))
    amax = np.abs(blocks).max(-1, keepdims=True)
    byte = np.maximum(np.where(amax > 0, np.frexp(amax)[1] - 1 + 127, 0) - down, 1)
    scale = np.exp2(byte - 127.0)
    codes = (blocks / scale).astype(np.float32).astype(dtype).astype(np.float64)
    return np.moveaxis((codes * scale).reshape(v.shape), -1, axis)


WIDE = False


def mx_kscale(k):
    if not WIDE:
        return np.ones(k)
    levels = np.array([10, -10, 5, -5, 0])
    if k % 512:
        return np.exp2(np.random.permutation(np.resize(levels, k // 32))).repeat(32)
    a = np.empty((k // 512, 16))
    for p in range(k // 512):
        a[p, :8] = np.random.permutation(np.resize(levels, 8))
        for g in range(8):
            far = levels[np.abs(levels - a[p, g]) >= 10]
            a[p, g + 8] = far[np.random.randint(len(far))]
    return np.exp2(a.ravel()).repeat(32)


def f64(x):
    return np.asarray(x).astype(np.float64)


def striped(idx):
    return np.tile(idx.reshape(-1, 16).T, (8, 1)).astype(np.uint16)


def unstriped(offs):
    return offs[:16].T.reshape(-1).astype(np.int64)


def striped8(idx):
    return np.concatenate([x.reshape(-1, 16).T for x in idx]).astype(np.uint16)


def runs(offs, k):
    lists = np.stack([offs[16 * r : 16 * r + 16].T.reshape(-1) for r in range(8)]).astype(np.int64)
    return lists[np.arange(k) % 512 // 64]


def pack_weight(w):
    k, n = w.shape
    w = f64(np.asarray(w, np.float32).astype(ml_dtypes.bfloat16)).reshape(k // 32, 32, n)
    amax = np.abs(w).max(1)
    byte = np.clip(np.where(amax > 0, np.frexp(amax)[1] - 1 + 127 - 7, 1), 1, 254)
    scaled = (w * np.exp2(127.0 - byte)[:, None, :]).reshape(k, n).astype(np.float32)
    words = np.ascontiguousarray(scaled.reshape(k // 512, 128, 4, n).transpose(0, 1, 3, 2)).astype(ml_dtypes.float8_e4m3fn).view(np.uint8)
    return words, np.ascontiguousarray(byte.astype(np.uint8).reshape(k // 512, 16, n))


def unpack_weight(words, scales):
    g, p, n, _ = words.shape
    vals = np.ascontiguousarray(words).view(ml_dtypes.float8_e4m3fn).astype(np.float64) * np.repeat(np.exp2(scales.astype(np.float64) - 127.0), 8, axis=1)[..., None]
    return vals.transpose(0, 1, 3, 2).reshape(g * 512, n)

def planes(y):
    n, m = y.shape
    v = y.astype(np.float32).astype(ml_dtypes.bfloat16).astype(np.float64).reshape(n // 32, 32, m)
    top = np.abs(v).max(1)
    byte = np.clip(np.where(top > 0, np.frexp(top)[1] - 1 + 127 - 7, 1), 1, 254)
    codes = (v * np.exp2(127.0 - byte)[:, None, :]).reshape(n, m).astype(np.float32).astype(ml_dtypes.float8_e4m3fn).view(np.uint8)
    words = codes.reshape(n // 512, 128, 4, m).transpose(0, 1, 3, 2)
    return np.ascontiguousarray(words), np.ascontiguousarray(byte.astype(np.uint8).reshape(n // 512, 16, m))


K, T, S, N, H, W, G, U = 512, 2048, 256, 512, 512, 192, 2048, 128


def setup_inputs():
    n = np.random.standard_normal
    s = mx_kscale(K)[:, None]
    u = mx_kscale(K)
    packed_xT = pack_weight(n((K, T)) * s)
    packed_w1 = pack_weight(n((K, H)) / np.sqrt(K) / s)
    packed_w2 = pack_weight(n((H, N)) / np.sqrt(H) / u[:, None])
    packed_dT = pack_weight(n((K, G)) / s)
    return {
        "x_words": packed_xT[0],
        "x_scales": packed_xT[1],
        "w1_words": packed_w1[0],
        "w1_scales": packed_w1[1],
        "gn": (np.random.uniform(0.5, 1.5, (H, 1)) * u[:, None]).astype(np.float32),
        "w2_words": packed_w2[0],
        "w2_scales": packed_w2[1],
        "d_words": packed_dT[0],
        "d_scales": packed_dT[1],
        "offs": striped(np.random.permutation(T)[:S]),
        "n1": striped(np.random.permutation(S)[:W]),
        "n2": striped(np.random.permutation(S)[:W]),
        "two": striped(np.random.permutation(T)[:S]),
        "k1": striped8(np.random.randint(0, G, (8, H))),
        "n3": striped(np.random.permutation(S)[:U]),
        "n4": striped(np.random.permutation(S)[:U]),
    }


def reference(x_words, x_scales, w1_words, w1_scales, gn, w2_words, w2_scales, d_words, d_scales, offs, n1, n2, two, k1, n3, n4):
    d_k1 = unpack_weight(d_words, d_scales)[np.arange(K)[:, None], runs(k1, K)]
    x_two = unpack_weight(x_words, x_scales)[:, unstriped(two)]
    b = 0.0625 * (d_k1.T @ x_two)
    xq = unpack_weight(x_words, x_scales)[:, unstriped(offs)]
    y = unpack_weight(w1_words, w1_scales).T @ xq
    old = y[:, unstriped(n1)]
    pa = y[:, unstriped(n2)]
    ra = old - (0.5 * pa)
    ds = y.copy()
    ds[:, unstriped(n1)] = ra
    z = f64(gn) * ds
    a = unpack_weight(w2_words, w2_scales).T @ mxq(z, 0, "e4m3")
    ra2 = b[:, unstriped(n4)] - (0.5 * a[:, unstriped(n3)])
    out = a.copy()
    out[:, unstriped(n3)] = ra2
    return (out,) + planes(out)

@@ -1,0 +1,191 @@
+from contextlib import ExitStack
+
+import concourse.mybir as mybir
+
+K, T, S, N, H, W, G, U = 512, 2048, 256, 512, 512, 192, 2048, 128
+FLOPS = 3 * 2 * 512 * 512 * 256
+
+F32 = mybir.dt.float32
+BF16 = mybir.dt.bfloat16
+I32 = mybir.dt.int32
+U32 = mybir.dt.uint32
+U16 = mybir.dt.uint16
+U8 = mybir.dt.uint8
+FP8X4 = mybir.dt.float8_e4m3fn_x4
+COPY = mybir.ActivationFunctionType.Copy
+MULT = mybir.AluOpType.mult
+ADD = mybir.AluOpType.add
+
+P = 128
+PACK = 4
+QUAD = 32
+
+
+def tile_picked_cdjoinputbkdif_none_po_kernel(
+    tc, x_words, x_scales, w1_words, w1_scales, gn, w2_words, w2_scales, d_words, d_scales,
+    offs, n1, n2, two, k1, n3, n4, out_0, out_1, out_2,
+):
+    nc = tc.nc
+    with ExitStack() as ctx:
+        lists = ctx.enter_context(tc.tile_pool(name="lists", bufs=1))
+        keep = ctx.enter_context(tc.tile_pool(name="keep", bufs=1))
+        psum = ctx.enter_context(tc.psum_pool(name="psum", bufs=1))
+
+        def load_list(name, src):
+            tile = lists.tile([P, src.shape[1]], U16, name=name)
+            nc.sync.dma_start(tile[:], src)
+            return tile
+
+        def load_words(name, src, queue):
+            tile = keep.tile([P, src.shape[2]], I32, name=name, align_bytes=64)
+            queue.dma_start(out=tile[:], in_=src[0].rearrange("p n t -> p (n t)").bitcast(I32))
+            return tile
+
+        def zeroed_bytes(name, width, engine):
+            tile = keep.tile([P, width], U8, name=name, align_bytes=64)
+            engine.memset(tile[:].bitcast(I32), 0)
+            return tile
+
+        def load_plane(tile, src, queues):
+            for q in range(PACK):
+                queues[q].dma_start(
+                    out=tile[QUAD * q : QUAD * q + PACK, :].bitcast(I32),
+                    in_=src[0, PACK * q : PACK * q + PACK, :].bitcast(I32),
+                )
+
+        def gather_codes(name, table, offsets, count, dtype):
+            tile = keep.tile([P, count], dtype, name=name, align_bytes=64)
+            nc.vector.tensor_copy(tile[:], table.indirect(offsets[:]))
+            return tile
+
+        def deal(name, src, dtype):
+            tile = keep.tile([P, H], dtype, name=name, align_bytes=64)
+            nc.vector.tensor_copy(
+                tile[:].rearrange("p (t m) -> p t m", t=PACK), src.rearrange("p (m t) -> p t m", t=PACK)
+            )
+            return tile
+
+        def product(name, tag, lw, ls, rw, rs):
+            bank = psum.tile([P, S], F32, name=name, tag=tag)
+            nc.tensor.matmul_mx(
+                out=bank[:], lhsT=lw.bitcast(FP8X4), lhsT_scale=ls,
+                rhs=rw[:].bitcast(FP8X4), rhs_scale=rs[:], start=True, stop=True,
+            )
+            return bank
+
+        def fetch(name, window, offsets, count):
+            tile = keep.tile([P, count], F32, name=name, align_bytes=64)
+            nc.scalar.activation(tile[:], window[:].indirect(offsets[:]), COPY)
+            return tile
+
+        xs = zeroed_bytes("xs", T, nc.vector)
+        w1s = zeroed_bytes("w1s", H, nc.gpsimd)
+        dsc = zeroed_bytes("dsc", G, nc.vector)
+        w2s = zeroed_bytes("w2s", N, nc.vector)
+        offs_l = load_list("offs_l", offs)
+        n1_l = load_list("n1_l", n1)
+        n2_l = load_list("n2_l", n2)
+        xw = load_words("xw", x_words, nc.sync)
+        load_plane(xs, x_scales, [nc.scalar] * 4)
+        load_plane(w1s, w1_scales, [nc.gpsimd, nc.gpsimd, nc.scalar, nc.scalar])
+        w1w = load_words("w1w", w1_words, nc.sync)
+        two_l = load_list("two_l", two)
+        k1_l = load_list("k1_l", k1)
+        for e in range(2):
+            nc.sync.dma_start(out=dsc[e:P:16, :].bitcast(I32), in_=d_scales[0, e:16:2, :].bitcast(I32))
+        dw = load_words("dw", d_words, nc.sync)
+        gain = keep.tile([P, PACK], F32, name="gain")
+        nc.sync.dma_start(out=gain[:], in_=gn.rearrange("(p t) o -> p (t o)", t=PACK))
+        load_plane(w2s, w2_scales, [nc.sync] * 4)
+        w2w = load_words("w2w", w2_words, nc.sync)
+        n4_l = load_list("n4_l", n4)
+        n3_l = load_list("n3_l", n3)
+
+        xq_s = gather_codes("xq_s", xs[:], offs_l, S, U8)
+        w1s_d = deal("w1s_d", w1s[:], U8)
+        xq_w = gather_codes("xq_w", xw[:].bitcast(U32), offs_l, S, U32)
+        y, old, pa = [], [], []
+        for t in range(PACK):
+            w1w_t = keep.tile([P, P], I32, name="w1w_d%d" % t, align_bytes=64)
+            nc.vector.tensor_copy(w1w_t[:], w1w[:, t:H:PACK])
+            bank = product("y_ps%d" % t, "bank%d" % t, w1w_t[:], w1s_d[:, P * t : P * (t + 1)], xq_w, xq_s)
+            y_t = keep.tile([P, S], F32, name="y%d" % t, align_bytes=64)
+            if t == 0:
+                nc.scalar.copy(y_t[:], bank[:])
+            else:
+                nc.vector.tensor_copy(y_t[:], bank[:])
+            y.append(y_t)
+            old.append(fetch("old%d" % t, y_t, n1_l, W))
+            pa.append(fetch("pa%d" % t, y_t, n2_l, W))
+
+        xt_s = gather_codes("xt_s", xs[:], two_l, S, U8)
+        xt_w = gather_codes("xt_w", xw[:].bitcast(U32), two_l, S, U32)
+        dk_s = gather_codes("dk_s", dsc[:], k1_l, H, U8)
+        dk_sd = deal("dk_sd", dk_s[:], U8)
+        for e in range(2):
+            nc.sync.dma_start(out=dk_sd[2 + e : P : QUAD, :].bitcast(I32), in_=dk_sd[16 + e : P : QUAD, :].bitcast(I32))
+        dk_w = gather_codes("dk_w", dw[:].bitcast(U32), k1_l, H, U32)
+        dk_wd = deal("dk_wd", dk_w[:], U32)
+        b = []
+        for t in range(PACK):
+            cols = slice(P * t, P * (t + 1))
+            bank = product("b_ps%d" % t, "bbank%d" % t, dk_wd[:, cols], dk_sd[:, cols], xt_w, xt_s)
+            b_t = keep.tile([P, S], F32, name="b%d" % t, align_bytes=64)
+            nc.vector.tensor_scalar(b_t[:], bank[:], 0.0625, None, MULT)
+            b.append(b_t)
+        w2s_d = deal("w2s_d", w2s[:], U8)
+        w2w_d = deal("w2w_d", w2w[:], I32)
+
+        HALF = S // 2
+        halves = [slice(0, HALF), slice(HALF, S)]
+
+        def quantise(words, scales, grouped):
+            for h in range(2):
+                nc.vector.quantize_mx(
+                    out=words[:, halves[h]].bitcast(FP8X4), scales=scales[:, halves[h]],
+                    in_=grouped[h][:].rearrange("p s t -> p (s t)"),
+                )
+
+        zb = [keep.tile([P, HALF, PACK], BF16, name="zb%d" % h, align_bytes=64) for h in range(2)]
+        for t in range(PACK):
+            ra = keep.tile([P, W], F32, name="ra%d" % t, align_bytes=64)
+            nc.vector.scalar_tensor_tensor(ra[:], pa[t][:], -0.5, old[t][:], MULT, ADD)
+            nc.scalar.activation(y[t][:].indirect(n1_l[:]), ra[:], COPY)
+            for h in range(2):
+                nc.vector.tensor_scalar(zb[h][:, :, t], y[t][:, halves[h]], gain[:, t : t + 1], None, MULT)
+        zw = keep.tile([P, S], U32, name="zw", align_bytes=64)
+        zs = keep.tile([P, S], U8, name="zs", align_bytes=64)
+        quantise(zw, zs, zb)
+
+        bg = [fetch("bg%d" % t, b[t], n4_l, U) for t in range(PACK)]
+
+        a, ag = [], []
+        for t in range(PACK):
+            cols = slice(P * t, P * (t + 1))
+            bank = product("a_ps%d" % t, "bank%d" % t, w2w_d[:, cols], w2s_d[:, cols], zw, zs)
+            a_t = keep.tile([P, S], F32, name="a%d" % t, align_bytes=64)
+            if t == 0:
+                nc.scalar.copy(a_t[:], bank[:])
+            else:
+                nc.vector.tensor_copy(a_t[:], bank[:])
+            a.append(a_t)
+            ag.append(fetch("ag%d" % t, a_t, n3_l, U))
+        ob = [keep.tile([P, HALF, PACK], BF16, name="ob%d" % h, align_bytes=64) for h in range(2)]
+        out_rows = out_0.rearrange("(p t) s -> p t s", t=PACK)
+        for t in range(PACK):
+            ra2 = keep.tile([P, U], F32, name="rb%d" % t, align_bytes=64)
+            nc.vector.scalar_tensor_tensor(ra2[:], ag[t][:], -0.5, bg[t][:], MULT, ADD)
+            nc.scalar.activation(a[t][:].indirect(n3_l[:]), ra2[:], COPY)
+            for h in range(2):
+                nc.vector.tensor_copy(ob[h][:, :, t], a[t][:, halves[h]])
+            nc.sync.dma_start(out=out_rows[:, t, :], in_=a[t][:])
+        ow = keep.tile([P, S], I32, name="ow", align_bytes=64)
+        osc = keep.tile([P, S], U8, name="osc", align_bytes=64)
+        quantise(ow, osc, ob)
+        nc.sync.dma_start(out=out_1[0].rearrange("p n t -> p (n t)").bitcast(I32), in_=ow[:])
+        for q in range(PACK):
+            queue = nc.scalar if q % 2 == 0 else nc.sync
+            queue.dma_start(
+                out=out_2[0, PACK * q : PACK * q + PACK, :].bitcast(I32),
+                in_=osc[QUAD * q : QUAD * q + PACK, :].bitcast(I32),
+            )

@@ -36,30 +36,30 @@ def tile_picked_cdjoinputbkdif_none_po_kernel(
             nc.sync.dma_start(tile[:], src)
             return tile
 
-        def load_words(name, src, queue):
-            tile = keep.tile([P, src.shape[2]], I32, name=name, align_bytes=64)
+        def load_words(name, src, queue, tag=None):
+            tile = keep.tile([P, src.shape[2]], I32, name=name, tag=tag or name, align_bytes=64)
             queue.dma_start(out=tile[:], in_=src[0].rearrange("p n t -> p (n t)").bitcast(I32))
             return tile
 
         def zeroed_bytes(name, width, engine):
-            tile = keep.tile([P, width], U8, name=name, align_bytes=64)
+            tile = keep.tile([P, width], U8, name=name, tag=name, align_bytes=64)
             engine.memset(tile[:].bitcast(I32), 0)
             return tile
 
-        def load_plane(tile, src, queues):
-            for q in range(PACK):
-                queues[q].dma_start(
+        def load_plane(tile, src, quadrants, queue):
+            for q in quadrants:
+                queue.dma_start(
                     out=tile[QUAD * q : QUAD * q + PACK, :].bitcast(I32),
                     in_=src[0, PACK * q : PACK * q + PACK, :].bitcast(I32),
                 )
 
-        def gather_codes(name, table, offsets, count, dtype):
-            tile = keep.tile([P, count], dtype, name=name, align_bytes=64)
+        def gather_codes(name, table, offsets, count, dtype, tag=None):
+            tile = keep.tile([P, count], dtype, name=name, tag=tag or name, align_bytes=64)
             nc.vector.tensor_copy(tile[:], table.indirect(offsets[:]))
             return tile
 
-        def deal(name, src, dtype):
-            tile = keep.tile([P, H], dtype, name=name, align_bytes=64)
+        def deal(name, src, dtype, tag=None):
+            tile = keep.tile([P, H], dtype, name=name, tag=tag or name, align_bytes=64)
             nc.vector.tensor_copy(
                 tile[:].rearrange("p (t m) -> p t m", t=PACK), src.rearrange("p (m t) -> p t m", t=PACK)
             )
@@ -78,37 +78,49 @@ def tile_picked_cdjoinputbkdif_none_po_kernel(
             nc.scalar.activation(tile[:], window[:].indirect(offsets[:]), COPY)
             return tile
 
-        xs = zeroed_bytes("xs", T, nc.vector)
-        w1s = zeroed_bytes("w1s", H, nc.gpsimd)
+        xs = keep.tile([P, T], U8, name="xs", tag="xs", align_bytes=64)
+        nc.gpsimd.memset(xs[:, 0 : T // 2].bitcast(I32), 0)
+        nc.vector.memset(xs[:, T // 2 : T].bitcast(I32), 0)
+        w1s = zeroed_bytes("w1s", H, nc.vector)
         dsc = zeroed_bytes("dsc", G, nc.vector)
         w2s = zeroed_bytes("w2s", N, nc.vector)
         offs_l = load_list("offs_l", offs)
-        n1_l = load_list("n1_l", n1)
-        n2_l = load_list("n2_l", n2)
-        xw = load_words("xw", x_words, nc.sync)
-        load_plane(xs, x_scales, [nc.scalar] * 4)
-        load_plane(w1s, w1_scales, [nc.gpsimd, nc.gpsimd, nc.scalar, nc.scalar])
         w1w = load_words("w1w", w1_words, nc.sync)
         two_l = load_list("two_l", two)
+        xw = load_words("xw", x_words, nc.sync)
+        load_plane(xs, x_scales, range(4), nc.scalar)
+        load_plane(w1s, w1_scales, range(4), nc.scalar)
+        n1_l = load_list("n1_l", n1)
+        n2_l = load_list("n2_l", n2)
         k1_l = load_list("k1_l", k1)
         for e in range(2):
             nc.sync.dma_start(out=dsc[e:P:16, :].bitcast(I32), in_=d_scales[0, e:16:2, :].bitcast(I32))
         dw = load_words("dw", d_words, nc.sync)
+        w2w = load_words("w2w", w2_words, nc.sync, "w2w")
+        load_plane(w2s, w2_scales, range(4), nc.sync)
         gain = keep.tile([P, PACK], F32, name="gain")
         nc.sync.dma_start(out=gain[:], in_=gn.rearrange("(p t) o -> p (t o)", t=PACK))
-        load_plane(w2s, w2_scales, [nc.sync] * 4)
-        w2w = load_words("w2w", w2_words, nc.sync)
         n4_l = load_list("n4_l", n4)
         n3_l = load_list("n3_l", n3)
 
         xq_s = gather_codes("xq_s", xs[:], offs_l, S, U8)
-        w1s_d = deal("w1s_d", w1s[:], U8)
-        xq_w = gather_codes("xq_w", xw[:].bitcast(U32), offs_l, S, U32)
+        xt_s = gather_codes("xt_s", xs[:], two_l, S, U8)
+        xq_w = gather_codes("xq_w", xw[:].bitcast(U32), offs_l, S, U32, "xs")
+
+        def deal_part(name, src, dtype, lo, hi):
+            tile = keep.tile([P, (hi - lo) * P], dtype, name=name, align_bytes=64)
+            nc.vector.tensor_copy(
+                tile[:].rearrange("p (t m) -> p t m", m=P), src.rearrange("p (m t) -> p t m", t=PACK)[:, lo:hi, :]
+            )
+            return [tile[:, P * i : P * (i + 1)] for i in range(hi - lo)]
+
+        w1w_d = deal_part("w1w_a", w1w[:], I32, 0, PACK)
+        w1s_d = deal_part("w1s_a", w1s[:], U8, 0, 1)
         y, old, pa = [], [], []
         for t in range(PACK):
-            w1w_t = keep.tile([P, P], I32, name="w1w_d%d" % t, align_bytes=64)
-            nc.vector.tensor_copy(w1w_t[:], w1w[:, t:H:PACK])
-            bank = product("y_ps%d" % t, "bank%d" % t, w1w_t[:], w1s_d[:, P * t : P * (t + 1)], xq_w, xq_s)
+            if t == 1:
+                w1s_d.extend(deal_part("w1s_b", w1s[:], U8, 1, PACK))
+            bank = product("y_ps%d" % t, "bank%d" % t, w1w_d[t], w1s_d[t], xq_w, xq_s)
             y_t = keep.tile([P, S], F32, name="y%d" % t, align_bytes=64)
             if t == 0:
                 nc.scalar.copy(y_t[:], bank[:])
@@ -118,20 +130,29 @@ def tile_picked_cdjoinputbkdif_none_po_kernel(
             old.append(fetch("old%d" % t, y_t, n1_l, W))
             pa.append(fetch("pa%d" % t, y_t, n2_l, W))
 
-        xt_s = gather_codes("xt_s", xs[:], two_l, S, U8)
-        xt_w = gather_codes("xt_w", xw[:].bitcast(U32), two_l, S, U32)
-        dk_s = gather_codes("dk_s", dsc[:], k1_l, H, U8)
+        dk_s = gather_codes("dk_s", dsc[:], k1_l, H, U8, "dk_s")
         dk_sd = deal("dk_sd", dk_s[:], U8)
         for e in range(2):
             nc.sync.dma_start(out=dk_sd[2 + e : P : QUAD, :].bitcast(I32), in_=dk_sd[16 + e : P : QUAD, :].bitcast(I32))
-        dk_w = gather_codes("dk_w", dw[:].bitcast(U32), k1_l, H, U32)
-        dk_wd = deal("dk_wd", dk_w[:], U32)
+        xt_w = gather_codes("xt_w", xw[:].bitcast(U32), two_l, S, U32)
+        dk_w = gather_codes("dk_w", dw[:].bitcast(U32), k1_l, H, U32, "dk_w")
+        dk_wd = deal("dk_wd", dk_w[:], U32, "dk_wd")
+
+        ra_tags = [None, None, "dk_s", "dk_w"]
+        for t in range(PACK):
+            ra = keep.tile([P, W], F32, name="ra%d" % t, tag=ra_tags[t] or "ra%d" % t, align_bytes=64)
+            nc.vector.scalar_tensor_tensor(ra[:], pa[t][:], -0.5, old[t][:], MULT, ADD)
+            nc.scalar.activation(y[t][:].indirect(n1_l[:]), ra[:], COPY)
+
         b = []
         for t in range(PACK):
             cols = slice(P * t, P * (t + 1))
             bank = product("b_ps%d" % t, "bbank%d" % t, dk_wd[:, cols], dk_sd[:, cols], xt_w, xt_s)
-            b_t = keep.tile([P, S], F32, name="b%d" % t, align_bytes=64)
-            nc.vector.tensor_scalar(b_t[:], bank[:], 0.0625, None, MULT)
+            b_t = keep.tile([P, S], F32, name="b%d" % t, tag="dk_w" if t == 2 else "b%d" % t, align_bytes=64)
+            if t < 2:
+                nc.vector.tensor_scalar(b_t[:], bank[:], 0.0625, None, MULT)
+            else:
+                nc.scalar.activation(b_t[:], bank[:], COPY, scale=0.0625)
             b.append(b_t)
         w2s_d = deal("w2s_d", w2s[:], U8)
         w2w_d = deal("w2w_d", w2w[:], I32)
@@ -146,11 +167,8 @@ def tile_picked_cdjoinputbkdif_none_po_kernel(
                     in_=grouped[h][:].rearrange("p s t -> p (s t)"),
                 )
 
-        zb = [keep.tile([P, HALF, PACK], BF16, name="zb%d" % h, align_bytes=64) for h in range(2)]
+        zb = [keep.tile([P, HALF, PACK], BF16, name="zb%d" % h, tag=["dk_wd", "xt_w"][h], align_bytes=64) for h in range(2)]
         for t in range(PACK):
-            ra = keep.tile([P, W], F32, name="ra%d" % t, align_bytes=64)
-            nc.vector.scalar_tensor_tensor(ra[:], pa[t][:], -0.5, old[t][:], MULT, ADD)
-            nc.scalar.activation(y[t][:].indirect(n1_l[:]), ra[:], COPY)
             for h in range(2):
                 nc.vector.tensor_scalar(zb[h][:, :, t], y[t][:, halves[h]], gain[:, t : t + 1], None, MULT)
         zw = keep.tile([P, S], U32, name="zw", align_bytes=64)

@@ -60,8 +60,10 @@ def tile_picked_cdjoinputbkdif_none_po_kernel(
 
         def deal(name, src, dtype, tag=None):
             tile = keep.tile([P, H], dtype, name=name, tag=tag or name, align_bytes=64)
+            run = 16 if dtype == U8 else 4
             nc.vector.tensor_copy(
-                tile[:].rearrange("p (t m) -> p t m", t=PACK), src.rearrange("p (m t) -> p t m", t=PACK)
+                tile[:].rearrange("p (t c i) -> p c t i", t=PACK, i=run),
+                src.rearrange("p (c i t) -> p c t i", t=PACK, i=run),
             )
             return tile
 
@@ -75,7 +77,7 @@ def tile_picked_cdjoinputbkdif_none_po_kernel(
 
         def fetch(name, window, offsets, count):
             tile = keep.tile([P, count], F32, name=name, align_bytes=64)
-            nc.scalar.activation(tile[:], window[:].indirect(offsets[:]), COPY)
+            nc.scalar.activation(tile[:], window.indirect(offsets[:]), COPY)
             return tile
 
         xs = keep.tile([P, T], U8, name="xs", tag="xs", align_bytes=64)
@@ -87,15 +89,16 @@ def tile_picked_cdjoinputbkdif_none_po_kernel(
         offs_l = load_list("offs_l", offs)
         w1w = load_words("w1w", w1_words, nc.sync)
         two_l = load_list("two_l", two)
+        load_plane(xs, x_scales, range(2, 4), nc.scalar)
+        load_plane(xs, x_scales, range(0, 2), nc.sync)
         xw = load_words("xw", x_words, nc.sync)
-        load_plane(xs, x_scales, range(4), nc.scalar)
-        load_plane(w1s, w1_scales, range(4), nc.scalar)
+        load_plane(w1s, w1_scales, range(4), nc.sync)
         n1_l = load_list("n1_l", n1)
         n2_l = load_list("n2_l", n2)
+        dw = load_words("dw", d_words, nc.sync)
         k1_l = load_list("k1_l", k1)
         for e in range(2):
             nc.sync.dma_start(out=dsc[e:P:16, :].bitcast(I32), in_=d_scales[0, e:16:2, :].bitcast(I32))
-        dw = load_words("dw", d_words, nc.sync)
         w2w = load_words("w2w", w2_words, nc.sync, "w2w")
         load_plane(w2s, w2_scales, range(4), nc.sync)
         gain = keep.tile([P, PACK], F32, name="gain")
@@ -107,15 +110,17 @@ def tile_picked_cdjoinputbkdif_none_po_kernel(
         xt_s = gather_codes("xt_s", xs[:], two_l, S, U8)
         xq_w = gather_codes("xq_w", xw[:].bitcast(U32), offs_l, S, U32, "xs")
 
-        def deal_part(name, src, dtype, lo, hi):
-            tile = keep.tile([P, (hi - lo) * P], dtype, name=name, align_bytes=64)
+        def deal_part(name, src, dtype, lo, hi, tag=None):
+            tile = keep.tile([P, (hi - lo) * P], dtype, name=name, tag=tag or name, align_bytes=64)
+            run = 16 if dtype == U8 else 4
             nc.vector.tensor_copy(
-                tile[:].rearrange("p (t m) -> p t m", m=P), src.rearrange("p (m t) -> p t m", t=PACK)[:, lo:hi, :]
+                tile[:].rearrange("p (t c i) -> p c t i", t=hi - lo, i=run),
+                src.rearrange("p (c i t) -> p c t i", t=PACK, i=run)[:, :, lo:hi, :],
             )
             return [tile[:, P * i : P * (i + 1)] for i in range(hi - lo)]
 
         w1w_d = deal_part("w1w_a", w1w[:], I32, 0, PACK)
-        w1s_d = deal_part("w1s_a", w1s[:], U8, 0, 1)
+        w1s_d = deal_part("w1s_a", w1s[:], U8, 0, 1, "xt_w")
         y, old, pa = [], [], []
         for t in range(PACK):
             if t == 1:
@@ -127,35 +132,39 @@ def tile_picked_cdjoinputbkdif_none_po_kernel(
             else:
                 nc.vector.tensor_copy(y_t[:], bank[:])
             y.append(y_t)
-            old.append(fetch("old%d" % t, y_t, n1_l, W))
-            pa.append(fetch("pa%d" % t, y_t, n2_l, W))
+            old.append(fetch("old%d" % t, y_t[:], n1_l, W))
+            pa.append(fetch("pa%d" % t, y_t[:], n2_l, W))
 
-        dk_s = gather_codes("dk_s", dsc[:], k1_l, H, U8, "dk_s")
+        def put_back(t, tag):
+            ra = keep.tile([P, W], F32, name="ra%d" % t, tag=tag, align_bytes=64)
+            nc.vector.scalar_tensor_tensor(ra[:], pa[t][:], -0.5, old[t][:], MULT, ADD)
+            nc.scalar.activation(y[t][:].indirect(n1_l[:]), ra[:], COPY)
+
+        dk_s = gather_codes("dk_s", dsc[:], k1_l, H, U8, "w1s")
         dk_sd = deal("dk_sd", dk_s[:], U8)
         for e in range(2):
             nc.sync.dma_start(out=dk_sd[2 + e : P : QUAD, :].bitcast(I32), in_=dk_sd[16 + e : P : QUAD, :].bitcast(I32))
         xt_w = gather_codes("xt_w", xw[:].bitcast(U32), two_l, S, U32)
-        dk_w = gather_codes("dk_w", dw[:].bitcast(U32), k1_l, H, U32, "dk_w")
+        put_back(0, "ra0")
+        dk_w = gather_codes("dk_w", dw[:].bitcast(U32), k1_l, H, U32, "w1s")
+        put_back(1, "dw")
         dk_wd = deal("dk_wd", dk_w[:], U32, "dk_wd")
-
-        ra_tags = [None, None, "dk_s", "dk_w"]
-        for t in range(PACK):
-            ra = keep.tile([P, W], F32, name="ra%d" % t, tag=ra_tags[t] or "ra%d" % t, align_bytes=64)
-            nc.vector.scalar_tensor_tensor(ra[:], pa[t][:], -0.5, old[t][:], MULT, ADD)
-            nc.scalar.activation(y[t][:].indirect(n1_l[:]), ra[:], COPY)
-
-        b = []
-        for t in range(PACK):
-            cols = slice(P * t, P * (t + 1))
-            bank = product("b_ps%d" % t, "bbank%d" % t, dk_wd[:, cols], dk_sd[:, cols], xt_w, xt_s)
-            b_t = keep.tile([P, S], F32, name="b%d" % t, tag="dk_w" if t == 2 else "b%d" % t, align_bytes=64)
-            if t < 2:
-                nc.vector.tensor_scalar(b_t[:], bank[:], 0.0625, None, MULT)
-            else:
-                nc.scalar.activation(b_t[:], bank[:], COPY, scale=0.0625)
-            b.append(b_t)
+        put_back(2, "w1s")
         w2s_d = deal("w2s_d", w2s[:], U8)
         w2w_d = deal("w2w_d", w2w[:], I32)
+        put_back(3, "w2w")
+
+        b_all = keep.tile([P, PACK * S], F32, name="b_all", tag="w2w", align_bytes=64)
+        for pair in range(2):
+            bank = psum.tile([P, 2 * S], F32, name="b_ps%d" % pair, tag="bbank%d" % pair)
+            for i in range(2):
+                cols = slice(P * (2 * pair + i), P * (2 * pair + i + 1))
+                nc.tensor.matmul_mx(
+                    out=bank[:, S * i : S * (i + 1)], lhsT=dk_wd[:, cols].bitcast(FP8X4), lhsT_scale=dk_sd[:, cols],
+                    rhs=xt_w[:].bitcast(FP8X4), rhs_scale=xt_s[:], start=True, stop=True,
+                )
+            nc.scalar.activation(b_all[:, 2 * S * pair : 2 * S * (pair + 1)], bank[:], COPY, scale=0.0625)
+        b = [b_all[:, S * t : S * (t + 1)] for t in range(PACK)]
 
         HALF = S // 2
         halves = [slice(0, HALF), slice(HALF, S)]
@@ -182,12 +191,9 @@ def tile_picked_cdjoinputbkdif_none_po_kernel(
             cols = slice(P * t, P * (t + 1))
             bank = product("a_ps%d" % t, "bank%d" % t, w2w_d[:, cols], w2s_d[:, cols], zw, zs)
             a_t = keep.tile([P, S], F32, name="a%d" % t, align_bytes=64)
-            if t == 0:
-                nc.scalar.copy(a_t[:], bank[:])
-            else:
-                nc.vector.tensor_copy(a_t[:], bank[:])
+            nc.vector.tensor_copy(a_t[:], bank[:])
             a.append(a_t)
-            ag.append(fetch("ag%d" % t, a_t, n3_l, U))
+            ag.append(fetch("ag%d" % t, a_t[:], n3_l, U))
         ob = [keep.tile([P, HALF, PACK], BF16, name="ob%d" % h, align_bytes=64) for h in range(2)]
         out_rows = out_0.rearrange("(p t) s -> p t s", t=PACK)
         for t in range(PACK):

@@ -95,12 +95,12 @@ def tile_picked_cdjoinputbkdif_none_po_kernel(
         load_plane(w1s, w1_scales, range(4), nc.sync)
         n1_l = load_list("n1_l", n1)
         n2_l = load_list("n2_l", n2)
-        dw = load_words("dw", d_words, nc.sync)
         k1_l = load_list("k1_l", k1)
         for e in range(2):
             nc.sync.dma_start(out=dsc[e:P:16, :].bitcast(I32), in_=d_scales[0, e:16:2, :].bitcast(I32))
-        w2w = load_words("w2w", w2_words, nc.sync, "w2w")
+        dw = load_words("dw", d_words, nc.sync)
         load_plane(w2s, w2_scales, range(4), nc.sync)
+        w2w = load_words("w2w", w2_words, nc.sync, "w2w")
         gain = keep.tile([P, PACK], F32, name="gain")
         nc.sync.dma_start(out=gain[:], in_=gn.rearrange("(p t) o -> p (t o)", t=PACK))
         n4_l = load_list("n4_l", n4)
@@ -124,7 +124,7 @@ def tile_picked_cdjoinputbkdif_none_po_kernel(
         y, old, pa = [], [], []
         for t in range(PACK):
             if t == 1:
-                w1s_d.extend(deal_part("w1s_b", w1s[:], U8, 1, PACK))
+                w1s_d.extend(deal_part("w1s_b", w1s[:], U8, 1, PACK, "dk_s"))
             bank = product("y_ps%d" % t, "bank%d" % t, w1w_d[t], w1s_d[t], xq_w, xq_s)
             y_t = keep.tile([P, S], F32, name="y%d" % t, align_bytes=64)
             if t == 0:
@@ -140,31 +140,35 @@ def tile_picked_cdjoinputbkdif_none_po_kernel(
             nc.vector.scalar_tensor_tensor(ra[:], pa[t][:], -0.5, old[t][:], MULT, ADD)
             nc.scalar.activation(y[t][:].indirect(n1_l[:]), ra[:], COPY)
 
-        dk_s = gather_codes("dk_s", dsc[:], k1_l, H, U8, "w1s")
+        dk_s = gather_codes("dk_s", dsc[:], k1_l, H, U8, "dk_s")
+        put_back(0, "ra0")
+        put_back(1, "dsc")
         dk_sd = deal("dk_sd", dk_s[:], U8)
         for e in range(2):
             nc.sync.dma_start(out=dk_sd[2 + e : P : QUAD, :].bitcast(I32), in_=dk_sd[16 + e : P : QUAD, :].bitcast(I32))
         xt_w = gather_codes("xt_w", xw[:].bitcast(U32), two_l, S, U32)
-        put_back(0, "ra0")
-        dk_w = gather_codes("dk_w", dw[:].bitcast(U32), k1_l, H, U32, "w1s")
-        put_back(1, "dw")
+        put_back(2, "dk_s")
+        dk_w = gather_codes("dk_w", dw[:].bitcast(U32), k1_l, H, U32, "dk_w")
+        put_back(3, "dw")
         dk_wd = deal("dk_wd", dk_w[:], U32, "dk_wd")
-        put_back(2, "w1s")
         w2s_d = deal("w2s_d", w2s[:], U8)
-        w2w_d = deal("w2w_d", w2w[:], I32)
-        put_back(3, "w2w")
+        w2w_d = deal("w2w_d", w2w[:], I32, "dk_w")
 
-        b_all = keep.tile([P, PACK * S], F32, name="b_all", tag="w2w", align_bytes=64)
-        for pair in range(2):
-            bank = psum.tile([P, 2 * S], F32, name="b_ps%d" % pair, tag="bbank%d" % pair)
-            for i in range(2):
-                cols = slice(P * (2 * pair + i), P * (2 * pair + i + 1))
+        b_all = keep.tile([P, 3 * S], F32, name="b_all", tag="dw", align_bytes=64)
+        b_last = keep.tile([P, S], F32, name="b_last", align_bytes=64)
+        b_banks = []
+        for g, members in enumerate([(0, 1), (2,), (3,)]):
+            bank = psum.tile([P, len(members) * S], F32, name="b_ps%d" % g, tag="bbank%d" % g)
+            for i, t in enumerate(members):
+                cols = slice(P * t, P * (t + 1))
                 nc.tensor.matmul_mx(
                     out=bank[:, S * i : S * (i + 1)], lhsT=dk_wd[:, cols].bitcast(FP8X4), lhsT_scale=dk_sd[:, cols],
                     rhs=xt_w[:].bitcast(FP8X4), rhs_scale=xt_s[:], start=True, stop=True,
                 )
-            nc.scalar.activation(b_all[:, 2 * S * pair : 2 * S * (pair + 1)], bank[:], COPY, scale=0.0625)
-        b = [b_all[:, S * t : S * (t + 1)] for t in range(PACK)]
+            b_banks.append(bank)
+        nc.scalar.activation(b_all[:, 0 : 2 * S], b_banks[0][:], COPY, scale=0.0625)
+        nc.scalar.activation(b_all[:, 2 * S : 3 * S], b_banks[1][:], COPY, scale=0.0625)
+        b = [b_all[:, S * t : S * (t + 1)] for t in range(3)] + [b_last[:]]
 
         HALF = S // 2
         halves = [slice(0, HALF), slice(HALF, S)]
@@ -173,17 +177,20 @@ def tile_picked_cdjoinputbkdif_none_po_kernel(
             for h in range(2):
                 nc.vector.quantize_mx(
                     out=words[:, halves[h]].bitcast(FP8X4), scales=scales[:, halves[h]],
-                    in_=grouped[h][:].rearrange("p s t -> p (s t)"),
+                    in_=grouped[h].rearrange("p s t -> p (s t)"),
                 )
 
-        zb = [keep.tile([P, HALF, PACK], BF16, name="zb%d" % h, tag=["dk_wd", "xt_w"][h], align_bytes=64) for h in range(2)]
-        for t in range(PACK):
-            for h in range(2):
-                nc.vector.tensor_scalar(zb[h][:, :, t], y[t][:, halves[h]], gain[:, t : t + 1], None, MULT)
-        zw = keep.tile([P, S], U32, name="zw", align_bytes=64)
+        zb_all = keep.tile([P, S * PACK], BF16, name="zb_all", tag="w2w", align_bytes=64)
+        zb = [zb_all[:, HALF * PACK * h : HALF * PACK * (h + 1)].rearrange("p (s t) -> p s t", t=PACK) for h in range(2)]
+        for t in range(PACK - 1):
+            nc.vector.tensor_scalar(zb_all[:, t : S * PACK : PACK], y[t][:], gain[:, t : t + 1], None, MULT)
+        for h in range(2):
+            nc.vector.tensor_scalar(zb[h][:, :, PACK - 1], y[PACK - 1][:, halves[h]], gain[:, PACK - 1 : PACK], None, MULT)
+        zw = keep.tile([P, S], U32, name="zw", tag="dk_wd", align_bytes=64)
         zs = keep.tile([P, S], U8, name="zs", align_bytes=64)
         quantise(zw, zs, zb)
 
+        nc.vector.tensor_scalar(b_last[:], b_banks[2][:], 0.0625, None, MULT)
         bg = [fetch("bg%d" % t, b[t], n4_l, U) for t in range(PACK)]
 
         a, ag = [], []
@@ -205,7 +212,7 @@ def tile_picked_cdjoinputbkdif_none_po_kernel(
             nc.sync.dma_start(out=out_rows[:, t, :], in_=a[t][:])
         ow = keep.tile([P, S], I32, name="ow", align_bytes=64)
         osc = keep.tile([P, S], U8, name="osc", align_bytes=64)
-        quantise(ow, osc, ob)
+        quantise(ow, osc, [ob[0][:], ob[1][:]])
         nc.sync.dma_start(out=out_1[0].rearrange("p n t -> p (n t)").bitcast(I32), in_=ow[:])
         for q in range(PACK):
             queue = nc.scalar if q % 2 == 0 else nc.sync

from contextlib import ExitStack

import concourse.mybir as mybir

K, T, S, N, H, W, G, U = 512, 2048, 256, 512, 512, 192, 2048, 128
FLOPS = 3 * 2 * 512 * 512 * 256

F32 = mybir.dt.float32
BF16 = mybir.dt.bfloat16
I32 = mybir.dt.int32
U32 = mybir.dt.uint32
U16 = mybir.dt.uint16
U8 = mybir.dt.uint8
FP8X4 = mybir.dt.float8_e4m3fn_x4
COPY = mybir.ActivationFunctionType.Copy
MULT = mybir.AluOpType.mult
ADD = mybir.AluOpType.add

P = 128
PACK = 4
QUAD = 32


def tile_picked_cdjoinputbkdif_none_po_kernel(
    tc, x_words, x_scales, w1_words, w1_scales, gn, w2_words, w2_scales, d_words, d_scales,
    offs, n1, n2, two, k1, n3, n4, out_0, out_1, out_2,
):
    nc = tc.nc
    with ExitStack() as ctx:
        lists = ctx.enter_context(tc.tile_pool(name="lists", bufs=1))
        keep = ctx.enter_context(tc.tile_pool(name="keep", bufs=1))
        psum = ctx.enter_context(tc.psum_pool(name="psum", bufs=1))

        def load_list(name, src):
            tile = lists.tile([P, src.shape[1]], U16, name=name)
            nc.sync.dma_start(tile[:], src)
            return tile

        def load_words(name, src, queue, tag=None):
            tile = keep.tile([P, src.shape[2]], I32, name=name, tag=tag or name, align_bytes=64)
            queue.dma_start(out=tile[:], in_=src[0].rearrange("p n t -> p (n t)").bitcast(I32))
            return tile

        def zeroed_bytes(name, width, engine):
            tile = keep.tile([P, width], U8, name=name, tag=name, align_bytes=64)
            engine.memset(tile[:].bitcast(I32), 0)
            return tile

        def load_plane(tile, src, quadrants, queue):
            for q in quadrants:
                queue.dma_start(
                    out=tile[QUAD * q : QUAD * q + PACK, :].bitcast(I32),
                    in_=src[0, PACK * q : PACK * q + PACK, :].bitcast(I32),
                )

        def gather_codes(name, table, offsets, count, dtype, tag=None):
            tile = keep.tile([P, count], dtype, name=name, tag=tag or name, align_bytes=64)
            nc.vector.tensor_copy(tile[:], table.indirect(offsets[:]))
            return tile

        def deal(name, src, dtype, tag=None):
            tile = keep.tile([P, H], dtype, name=name, tag=tag or name, align_bytes=64)
            run = 16 if dtype == U8 else 4
            nc.vector.tensor_copy(
                tile[:].rearrange("p (t c i) -> p c t i", t=PACK, i=run),
                src.rearrange("p (c i t) -> p c t i", t=PACK, i=run),
            )
            return tile

        def product(name, tag, lw, ls, rw, rs):
            bank = psum.tile([P, S], F32, name=name, tag=tag)
            nc.tensor.matmul_mx(
                out=bank[:], lhsT=lw.bitcast(FP8X4), lhsT_scale=ls,
                rhs=rw[:].bitcast(FP8X4), rhs_scale=rs[:], start=True, stop=True,
            )
            return bank

        def fetch(name, window, offsets, count):
            tile = keep.tile([P, count], F32, name=name, align_bytes=64)
            nc.scalar.activation(tile[:], window.indirect(offsets[:]), COPY)
            return tile

        xs = keep.tile([P, T], U8, name="xs", tag="xs", align_bytes=64)
        nc.gpsimd.memset(xs[:, 0 : T // 2].bitcast(I32), 0)
        nc.vector.memset(xs[:, T // 2 : T].bitcast(I32), 0)
        w1s = zeroed_bytes("w1s", H, nc.vector)
        dsc = zeroed_bytes("dsc", G, nc.vector)
        w2s = zeroed_bytes("w2s", N, nc.vector)
        offs_l = load_list("offs_l", offs)
        w1w = load_words("w1w", w1_words, nc.sync)
        two_l = load_list("two_l", two)
        load_plane(xs, x_scales, range(2, 4), nc.scalar)
        load_plane(xs, x_scales, range(0, 2), nc.sync)
        xw = load_words("xw", x_words, nc.sync)
        load_plane(w1s, w1_scales, range(4), nc.sync)
        n1_l = load_list("n1_l", n1)
        n2_l = load_list("n2_l", n2)
        k1_l = load_list("k1_l", k1)
        for e in range(2):
            nc.sync.dma_start(out=dsc[e:P:16, :].bitcast(I32), in_=d_scales[0, e:16:2, :].bitcast(I32))
        dw = load_words("dw", d_words, nc.sync)
        load_plane(w2s, w2_scales, range(4), nc.sync)
        w2w = load_words("w2w", w2_words, nc.sync, "w2w")
        gain = keep.tile([P, PACK], F32, name="gain")
        nc.sync.dma_start(out=gain[:], in_=gn.rearrange("(p t) o -> p (t o)", t=PACK))
        n4_l = load_list("n4_l", n4)
        n3_l = load_list("n3_l", n3)

        xq_s = gather_codes("xq_s", xs[:], offs_l, S, U8)
        xt_s = gather_codes("xt_s", xs[:], two_l, S, U8)
        xq_w = gather_codes("xq_w", xw[:].bitcast(U32), offs_l, S, U32, "xs")

        def deal_part(name, src, dtype, lo, hi, tag=None):
            tile = keep.tile([P, (hi - lo) * P], dtype, name=name, tag=tag or name, align_bytes=64)
            run = 16 if dtype == U8 else 4
            nc.vector.tensor_copy(
                tile[:].rearrange("p (t c i) -> p c t i", t=hi - lo, i=run),
                src.rearrange("p (c i t) -> p c t i", t=PACK, i=run)[:, :, lo:hi, :],
            )
            return [tile[:, P * i : P * (i + 1)] for i in range(hi - lo)]

        w1w_d = deal_part("w1w_a", w1w[:], I32, 0, PACK)
        w1s_d = deal_part("w1s_a", w1s[:], U8, 0, 1, "xt_w")
        y, old, pa = [], [], []
        for t in range(PACK):
            if t == 1:
                w1s_d.extend(deal_part("w1s_b", w1s[:], U8, 1, PACK, "dk_s"))
            bank = product("y_ps%d" % t, "bank%d" % t, w1w_d[t], w1s_d[t], xq_w, xq_s)
            y_t = keep.tile([P, S], F32, name="y%d" % t, align_bytes=64)
            if t == 0:
                nc.scalar.copy(y_t[:], bank[:])
            else:
                nc.vector.tensor_copy(y_t[:], bank[:])
            y.append(y_t)
            old.append(fetch("old%d" % t, y_t[:], n1_l, W))
            pa.append(fetch("pa%d" % t, y_t[:], n2_l, W))

        def put_back(t, tag):
            ra = keep.tile([P, W], F32, name="ra%d" % t, tag=tag, align_bytes=64)
            nc.vector.scalar_tensor_tensor(ra[:], pa[t][:], -0.5, old[t][:], MULT, ADD)
            nc.scalar.activation(y[t][:].indirect(n1_l[:]), ra[:], COPY)

        dk_s = gather_codes("dk_s", dsc[:], k1_l, H, U8, "dk_s")
        put_back(0, "ra0")
        put_back(1, "dsc")
        dk_sd = deal("dk_sd", dk_s[:], U8)
        for e in range(2):
            nc.sync.dma_start(out=dk_sd[2 + e : P : QUAD, :].bitcast(I32), in_=dk_sd[16 + e : P : QUAD, :].bitcast(I32))
        xt_w = gather_codes("xt_w", xw[:].bitcast(U32), two_l, S, U32)
        put_back(2, "dk_s")
        dk_w = gather_codes("dk_w", dw[:].bitcast(U32), k1_l, H, U32, "dk_w")
        put_back(3, "dw")
        dk_wd = deal("dk_wd", dk_w[:], U32, "dk_wd")
        w2s_d = deal("w2s_d", w2s[:], U8)
        w2w_d = deal("w2w_d", w2w[:], I32, "dk_w")

        b_all = keep.tile([P, 3 * S], F32, name="b_all", tag="dw", align_bytes=64)
        b_last = keep.tile([P, S], F32, name="b_last", align_bytes=64)
        b_banks = []
        for g, members in enumerate([(0, 1), (2,), (3,)]):
            bank = psum.tile([P, len(members) * S], F32, name="b_ps%d" % g, tag="bbank%d" % g)
            for i, t in enumerate(members):
                cols = slice(P * t, P * (t + 1))
                nc.tensor.matmul_mx(
                    out=bank[:, S * i : S * (i + 1)], lhsT=dk_wd[:, cols].bitcast(FP8X4), lhsT_scale=dk_sd[:, cols],
                    rhs=xt_w[:].bitcast(FP8X4), rhs_scale=xt_s[:], start=True, stop=True,
                )
            b_banks.append(bank)
        nc.scalar.activation(b_all[:, 0 : 2 * S], b_banks[0][:], COPY, scale=0.0625)
        nc.scalar.activation(b_all[:, 2 * S : 3 * S], b_banks[1][:], COPY, scale=0.0625)
        b = [b_all[:, S * t : S * (t + 1)] for t in range(3)] + [b_last[:]]

        HALF = S // 2
        halves = [slice(0, HALF), slice(HALF, S)]

        def quantise(words, scales, grouped):
            for h in range(2):
                nc.vector.quantize_mx(
                    out=words[:, halves[h]].bitcast(FP8X4), scales=scales[:, halves[h]],
                    in_=grouped[h].rearrange("p s t -> p (s t)"),
                )

        zb_all = keep.tile([P, S * PACK], BF16, name="zb_all", tag="w2w", align_bytes=64)
        zb = [zb_all[:, HALF * PACK * h : HALF * PACK * (h + 1)].rearrange("p (s t) -> p s t", t=PACK) for h in range(2)]
        for t in range(PACK - 1):
            nc.vector.tensor_scalar(zb_all[:, t : S * PACK : PACK], y[t][:], gain[:, t : t + 1], None, MULT)
        for h in range(2):
            nc.vector.tensor_scalar(zb[h][:, :, PACK - 1], y[PACK - 1][:, halves[h]], gain[:, PACK - 1 : PACK], None, MULT)
        zw = keep.tile([P, S], U32, name="zw", tag="dk_wd", align_bytes=64)
        zs = keep.tile([P, S], U8, name="zs", align_bytes=64)
        quantise(zw, zs, zb)

        nc.vector.tensor_scalar(b_last[:], b_banks[2][:], 0.0625, None, MULT)
        bg = [fetch("bg%d" % t, b[t], n4_l, U) for t in range(PACK)]

        a, ag = [], []
        for t in range(PACK):
            cols = slice(P * t, P * (t + 1))
            bank = product("a_ps%d" % t, "bank%d" % t, w2w_d[:, cols], w2s_d[:, cols], zw, zs)
            a_t = keep.tile([P, S], F32, name="a%d" % t, align_bytes=64)
            nc.vector.tensor_copy(a_t[:], bank[:])
            a.append(a_t)
            ag.append(fetch("ag%d" % t, a_t[:], n3_l, U))
        ob = [keep.tile([P, HALF, PACK], BF16, name="ob%d" % h, align_bytes=64) for h in range(2)]
        out_rows = out_0.rearrange("(p t) s -> p t s", t=PACK)
        for t in range(PACK):
            ra2 = keep.tile([P, U], F32, name="rb%d" % t, align_bytes=64)
            nc.vector.scalar_tensor_tensor(ra2[:], ag[t][:], -0.5, bg[t][:], MULT, ADD)
            nc.scalar.activation(a[t][:].indirect(n3_l[:]), ra2[:], COPY)
            for h in range(2):
                nc.vector.tensor_copy(ob[h][:, :, t], a[t][:, halves[h]])
            nc.sync.dma_start(out=out_rows[:, t, :], in_=a[t][:])
        ow = keep.tile([P, S], I32, name="ow", align_bytes=64)
        osc = keep.tile([P, S], U8, name="osc", align_bytes=64)
        quantise(ow, osc, [ob[0][:], ob[1][:]])
        nc.sync.dma_start(out=out_1[0].rearrange("p n t -> p (n t)").bitcast(I32), in_=ow[:])
        for q in range(PACK):
            queue = nc.scalar if q % 2 == 0 else nc.sync
            queue.dma_start(
                out=out_2[0, PACK * q : PACK * q + PACK, :].bitcast(I32),
                in_=osc[QUAD * q : QUAD * q + PACK, :].bitcast(I32),
            )
